import numpy as np, ml_dtypes
CORES = [25,29,65,69,153,157,193,197]
N = 8
import mx_ref
BF = ml_dtypes.bfloat16
def entries(a):
    return np.ascontiguousarray(a.T).reshape(-1)
def table(e):
    return np.ascontiguousarray(np.reshape(e, (-1, 16)).T).astype(np.int32)
def cols(t, e):
    v = np.concatenate([t.reshape(128, -1, 4), np.zeros((128, 1, 4), BF)], axis=1)
    return np.ascontiguousarray(v[:, e]).reshape(128, -1)
def tile(rs):
    return np.stack(rs, axis=2).reshape(128, -1).astype(BF)
def cut(t, i, w=512):
    return t[:, w * i:w * i + w]
def f(rng, *shape):
    return mx_ref.flush((rng.standard_normal(shape, dtype=np.float32) * np.exp2(rng.integers(-2, 3, shape[:-1] + (1,)))).astype(BF))
def wide(rng, *shape, cols=0):
    v = rng.standard_normal(shape, dtype=np.float32) * np.exp2(rng.integers(-12, 13, shape)).astype(np.float32)
    if cols: v *= np.repeat(np.exp2(rng.integers(-cols, cols + 1, shape[:-2] + (1, shape[-1] // 4))) * (rng.random(shape[:-2] + (1, shape[-1] // 4)) > 0.0625), 4, axis=-1).astype(np.float32)
    return mx_ref.flush(v.astype(BF))
T, CAPA, CAPB, TR = 512, 112, 96, 16
def mix(rng, n, la=0, lb=0):
    n = n.copy()
    for _ in range(4000):
        p, q = rng.integers(0, N, (2, 3)); k = rng.integers(0, 4)
        p2, q2 = p.copy(), q.copy(); m = n.copy()
        if k == 3: p2[1] = q[1]
        else: p2[k], q2[k] = q[k], p[k]
        m[tuple(p)] -= 1; m[tuple(p2)] += 1
        if k < 3: m[tuple(q)] -= 1; m[tuple(q2)] += 1
        sa, ab = m.sum(axis=2), m.sum(axis=0)
        if m.min() >= 0 and m.max() <= TR and (sa <= CAPA).all() and (sa >= la).all() and (ab <= CAPB).all() and (ab >= lb).all(): n = m
    return n
def even():
    return np.full((N, N, N), T // N ** 2)
def places(rng, k, cap, by=None):
    out = np.zeros(len(k), int)
    for g in np.unique(k):
        j = np.flatnonzero(k == g)
        if by is None: out[j] = g * cap + rng.permutation(cap)[:len(j)]
        else: out[j[np.argsort(by[j])]] = g * cap + cap - 1 - np.arange(len(j))
    return out
def lists(rng, n, back=False):
    s, a, b = np.repeat(np.argwhere(n >= 0), n.reshape(-1), axis=0).T
    col = np.concatenate([rng.permutation(T) for r in range(N)])
    snd, pas, tri = np.full(N * N * CAPA, -1), np.full(N * N * CAPB, -1), np.full(N * N * N * TR, -1)
    p1 = places(rng, s * N + a, CAPA, col if back else None); snd[p1] = col
    arr = s * CAPA + p1 % CAPA
    p2 = places(rng, a * N + b, CAPB, arr if back else None); pas[p2] = arr
    p3 = places(rng, (s * N + a) * N + b, TR, col if back else None); tri[p3] = col
    c, t = a * CAPB + p2 % CAPB, (s * N + a) * TR + p3 % TR
    plc, plt = [], []
    for r in range(N):
        j = rng.permutation(np.flatnonzero(b == r))
        if back: j = j[np.argsort(-c[j])]
        plc.append(table(c[j])); plt.append(table(t[j]))
    return {"snd": np.stack([table(v) for v in snd.reshape(N, -1)]), "pas": np.stack([table(v) for v in pas.reshape(N, -1)]), "tri": np.stack([table(v) for v in tri.reshape(N, -1)]), "plc": np.stack(plc), "plt": np.stack(plt)}
def values(rng):
    return {"x": f(rng, N, 128, 4 * T), "w": f(rng, N, 128, 2048), "vv": f(rng, N, 128, 512)}
def setup_inputs(rng):
    return {**values(rng), **lists(rng, mix(rng, even()))}
def heavy(rng, d):
    n = even()
    for k in range(CAPB // N - T // N ** 2):
        for s in range(N):
            for a in range(N):
                n[s, a, (a + d) % N] += 1; n[s, a, (a + d + 1 + (s + k) % (N - 1)) % N] -= 1
    return {**values(rng), **lists(rng, mix(rng, n, lb=CAPB * np.roll(np.eye(N, dtype=int), d, axis=1)))}
def setup_inputs_diag(rng):
    return heavy(rng, 0)
def setup_inputs_onward(rng):
    return heavy(rng, int(rng.integers(1, N)))
def setup_inputs_full(rng):
    k = T // CAPA
    g = np.zeros((N, N), int); g[:, :k] = CAPA; g[:, k] = T - k * CAPA
    g = np.stack([np.roll(g[s], s) for s in range(N)])[rng.permutation(N)][:, rng.permutation(N)]
    return {**values(rng), **lists(rng, mix(rng, np.repeat(g[:, :, None] // N, N, axis=2), la=np.where(g == CAPA, CAPA, 0)))}
def setup_inputs_reversed(rng):
    return {**values(rng), **lists(rng, mix(rng, even()), back=True)}
def setup_inputs_spread(rng):
    d = setup_inputs(rng); d["x"] = wide(rng, N, 128, 4 * T); return d
def check_inputs(d):
    b = []
    snd, pas, tri, plc, plt = [[entries(d[k][r]) for r in range(N)] for k in ("snd", "pas", "tri", "plc", "plt")]
    for r in range(N):
        if snd[r].min() < -1 or not np.array_equal(np.sort(snd[r][snd[r] >= 0]), np.arange(T)): b.append("snd")
        if tri[r].min() < -1 or not np.array_equal(np.sort(tri[r][tri[r] >= 0]), np.arange(T)): b.append("tri")
        for a in range(N):
            u, v = snd[r][a * CAPA:(a + 1) * CAPA], tri[r][a * N * TR:(a + 1) * N * TR]
            if not np.array_equal(np.sort(u[u >= 0]), np.sort(v[v >= 0])): b.append("tri")
    arrived = [np.concatenate([snd[s][a * CAPA:(a + 1) * CAPA] for s in range(N)]) for a in range(N)]
    for a in range(N):
        if pas[a].min() < -1 or not np.array_equal(np.sort(pas[a][pas[a] >= 0]), np.flatnonzero(arrived[a] >= 0)): b.append("pas")
    if b: return b
    for r in range(N):
        k = np.concatenate([pas[a][r * CAPB:(r + 1) * CAPB] for a in range(N)])
        t = np.concatenate([tri[s][(a * N + r) * TR:(a * N + r + 1) * TR] for s in range(N) for a in range(N)])
        if not np.array_equal(np.sort(plc[r]), np.flatnonzero(k >= 0)): b.append("plc"); continue
        if not np.array_equal(np.sort(plt[r]), np.flatnonzero(t >= 0)): b.append("plt"); continue
        a, m = plc[r] // CAPB, k[plc[r]]
        if (plt[r] // TR != m // CAPA * N + a).any() or (t[plt[r]] != np.stack(arrived)[a, m]).any(): b.append("plt")
    return b
def reference(x, w, vv, snd, pas, tri, plc, plt):
    h = []
    for a in range(N):
        q = mx_ref.quantize(np.concatenate([cols(x[s], entries(snd[s])[a * CAPA:(a + 1) * CAPA]) for s in range(N)], axis=1))
        h.append(tile([np.maximum(mx_ref.matmul(mx_ref.quantize(cut(w[a], i)), q), np.float32(0)) * np.float32(0.043) for i in range(4)]))
    y = np.zeros((N, 128, T), np.float32)
    for b in range(N):
        t = np.concatenate([cols(h[a], entries(pas[a])[b * CAPB:(b + 1) * CAPB]) for a in range(N)], axis=1)
        y[b] = mx_ref.matmul(mx_ref.quantize(vv[b]), mx_ref.quantize(cols(t, entries(plc[b]))))
    return {"y": y}

from concourse.bass import DstId, RemoteDMATransfer
from concourse.mybir import dt, AluOpType, ActivationFunctionType

Q8 = "float8_e4m3fn_x4"
SCRATCH = {
    "trs": ("sbuf", [128, 2, 2, 4, 4], "int32"),
    "off": ("sbuf", [128, 4, 16], "uint16"),
    "xs": ("sbuf", [128, 2048], "bfloat16"),
    "xg": ("sbuf", [128, 4096], "bfloat16"),
    "ws": ("sbuf", [128, 2048], "bfloat16"),
    "vs": ("sbuf", [128, 512], "bfloat16"),
    "xq": ("sbuf", [128, 1024], Q8), "xp": ("sbuf", [128, 1024], "uint8"),
    "wq": ("sbuf", [128, 512], Q8), "wp": ("sbuf", [128, 512], "uint8"),
    "vq": ("sbuf", [128, 128], Q8), "vp": ("sbuf", [128, 128], "uint8"),
    "rq": ("sbuf", [128, 256], Q8), "rp": ("sbuf", [128, 256], "uint8"),
    "nq": ("sbuf", [128, 256], Q8), "np": ("sbuf", [128, 256], "uint8"),
    "fq": ("sbuf", [128, 256], Q8), "fp": ("sbuf", [128, 256], "uint8"),
    "h": ("sbuf", [128, 4, 512], "bfloat16"),
    "hm": ("sbuf", [128, 4, 256], "bfloat16"),
    "hq": ("sbuf", [128, 512], Q8), "hp": ("sbuf", [128, 512], "uint8"),
    "yq": ("sbuf", [128, 1024], Q8), "yp": ("sbuf", [128, 1024], "uint8"),
    "pls": ("sbuf", [128, 32], "int32"),
    "pt": ("sbuf", [128, 10, 32], "int32"),
    "yo": ("sbuf", [128, 32], "uint16"),
    "ys": ("sbuf", [128, 1024], "float32"),
    "yb": ("sbuf", [128, 512], "float32"),
    "ps": ("psum", [128, 4096], "float32"),
}
SEMAPHORES = ["lt", "lx", "lw0", "lw", "lv", "lp", "lo", "ly", "cv", "cs", "ct", "snd",
              "w0", "w1", "rx0", "rx1", "jn", "jf", "y0", "y1", "y2"]
PLANE = {"xq": "xp", "wq": "wp", "rq": "rp", "nq": "np", "fq": "fp", "hq": "hp", "yq": "yp"}
N = 8


def make_plan(T, topo):
    C = T.cores
    par = [0 if topo.chip(C[r]) == topo.chip(C[0]) or topo.same_plane(C[r], C[0]) else 1 for r in range(N)]
    die = [0 if topo.die(C[r]) == topo.die(C[0]) else 1 for r in range(N)]
    hst = [0 if topo.host(C[r]) == topo.host(C[0]) else 1 for r in range(N)]
    at = {(hst[r], par[r], die[r]): r for r in range(N)}
    m1, m2 = [], []
    for r in range(N):
        far = [C[q] for q in range(N) if par[q] != par[r]][0]
        port = [c for c in topo.cores_of(C[r]) if topo.die(c) == topo.die(C[r]) and c != C[r] and topo.may_write(c, far)]
        m1.append(port[0])
        m2.append(port[1])
    S = {}
    for a in range(N):
        p, e, h = par[a], die[a], hst[a]
        near = [b for b in range(N) if par[b] == p]
        far = [b for b in range(N) if par[b] != p]
        me = 64 * (2 * h + e)
        S[C[a], "w0"] = [(m, "wq", 0, "wq", 0, 128, "w0") for m in (m1[a], m2[a])]
        S[C[a], "w1"] = [(m, "wq", 128, "wq", 128, 384, "w1") for m in (m1[a], m2[a])]
        S[C[a], "w2"] = [(m, "wp", 0, "wp", 0, 512, "w1") for m in (m1[a], m2[a])]
        for d in (0, 1):
            S[C[a], "xf%d" % d] = [(m, "xq", 256 * d + 128 * q, "rq", 128 * d, 128, "rx%d" % d) for q, m in ((0, m1[a]), (1, m2[a]))]
            for q, m in ((0, m1[a]), (1, m2[a])):
                to = [at[f, 1 - p, d] for f in (0, 1)]
                S[m, "x%d" % d] = [(C[t] if q == par[t] else m2[t], "rq", 128 * d + 64 * f, "fq", me, 64, "jf") for f, t in enumerate(to)]
        S[C[a], "xn"] = []
        for f in (0, 1):
            for d in (0, 1):
                t = at[f, p, d]
                for q in (0, 1):
                    if (t, q) != (a, p):
                        S[C[a], "xn"].append((C[t] if q == p else m1[t], "xq", 512 + 256 * d + 128 * q + 64 * f, "nq", me, 64, "jn"))
        S[C[a], "h"] = [(C[b], "hq", 128 * j, "yq", 128 * (2 * h + e), 128, "y0") for j, b in enumerate(near) if b != a]
        S[m1[a], "h"] = [(C[b], "hq", 64 * j, "yq", 512 + me, 64, "y1") for j, b in enumerate(far)]
        S[m2[a], "h"] = [(C[b], "hq", 64 * j, "yq", 768 + me, 64, "y2") for j, b in enumerate(far)]
    calls = {}
    for (c, st), moves in S.items():
        if st[0] == "w":
            calls[c, st] = moves
        else:
            calls[c, st + "c"] = moves
            calls[c, st + "s"] = [(d, PLANE[sb], sc, PLANE[db], dc, w, k) for d, sb, sc, db, dc, w, k in moves]
    return dict(C=C, par=par, die=die, hst=hst, at=at, m1=m1, m2=m2, S=calls)


def engines_of(core, moves, topo):
    own = topo.cores_of(core)
    off = [j for j, m in enumerate(moves) if m[0] not in own]
    on = [j for j, m in enumerate(moves) if m[0] in own]
    out = {}
    e_off = topo.engines(core, moves[off[0]][0]) if off else []
    for js, ok in ((off, e_off), (on, [k for k in topo.engines(core, moves[on[0]][0]) if k not in e_off] if on else [])):
        per = 1
        while js and 2 * per * len(js) <= len(ok):
            per *= 2
        for i, j in enumerate(js):
            out[j] = ok[per * i:per * i + per]
    return [out[j] for j in range(len(moves))]


def rank_program(g, core, T, topo):
    P = make_plan(T, topo)
    S, C, par, die, hst, at = P["S"], P["C"], P["par"], P["die"], P["hst"], P["at"]
    rank = T.rank_of(core)
    helper = [k for k in ("m1", "m2") if core in P[k]]
    if rank is None and not helper:
        return
    sem, V, A, X = T.sem, g.vector, g.scalar, g.tensor
    ACT, OP = ActivationFunctionType, AluOpType
    queue = {"cv": V, "cs": A}
    H = T.h if rank is not None else T.hm

    due = {}
    for (c, st), moves in S.items():
        for m, en in zip(moves, engines_of(c, moves, topo)):
            if m[0] == core:
                due[m[6]] = due.get(m[6], 0) + len(en)
    n = {"cv": 0, "cs": 0, "ct": 0, "snd": 0}

    def did(ins, s):
        ins.then_inc(sem[s], 1)
        n[s] += 1
        return n[s]

    def arrived(q, s):
        q.wait_ge(sem[s], due[s])

    def send(*calls):
        for st in calls:
            moves, tr = S[core, st], []
            for (d, sb, sc, db, dc, w, s), e in zip(moves, engines_of(core, moves, topo)):
                rid, pid = topo.addr(d, core)
                src, dst = T[sb][:, sc:sc + w], T[db][:, dc:dc + w]
                if sb in PLANE:
                    src, dst = src.bitcast(dt.uint8), dst.bitcast(dt.uint8)
                tr.append(RemoteDMATransfer(dst_ids=[DstId(rid=rid, pnc=pid)], dma_engine_mask=sum(1 << k for k in e),
                                            remote_sem=sem[s], srcs=[src], dsts=[dst]))
                n["snd"] += len(e)
            g.remote_dma_fused(tr, local_sem=sem.snd)

    def first_stage(src, w, bank0):
        k = [did(X.matmul_mx(T.ps[:, 512 * (bank0 + i):512 * (bank0 + i) + 256], T.wq[:, 128 * i:128 * i + 128], T.wp[:, 128 * i:128 * i + 128],
                             T[src][:, 0:256], T[PLANE[src]][:, 0:256], True, True), "ct") for i in range(4)]
        for i in range(4):
            s = ("cv", "cs")[i % 2]
            queue[s].wait_ge(sem.ct, k[i])
            for j in range(4):
                c, in_ = 4 * (w + 16 * j), T.ps[:, 512 * (bank0 + i) + 64 * j:512 * (bank0 + i) + 64 * j + 64]
                out = H[:, :, c + i:c + 64:4]
                if s == "cv":
                    did(V.tensor_scalar(out, in_, 0.0, 0.043, OP.max, OP.mult), "cv")
                else:
                    did(A.activation(out, in_, ACT.Relu, scale=0.043), "cs")

    def pack_h(w):
        V.wait_ge(sem.cv, n["cv"])
        V.wait_ge(sem.cs, n["cs"])
        return did(V.quantize_mx(T.hq[:, 0:4 * w], T.hp[:, 0:4 * w], H[:]), "cv")

    def finish():
        for s in ("cv", "cs", "ct", "snd"):
            if n[s]:
                g.wait_ge(sem[s], n[s])

    if rank is None:
        for d in (0, 1):
            arrived(g, "rx%d" % d), send("x%dc" % d, "x%ds" % d)
        arrived(X, "w0"), arrived(X, "w1")
        x, s = ("nq", "jn") if helper[0] == "m1" else ("fq", "jf")
        arrived(X, s)
        first_stage(x, 0, 0)
        g.wait_ge(sem.cv, pack_h(64))
        send("hc", "hs")
        return finish()

    p, e, h = par[rank], die[rank], hst[rank]
    g.scalar.dma_start(T.ws[:, 0:512], T.w[:, 0:512]).then_inc(sem.lw0, 16)
    for k in range(8):
        q = g.sync if k % 2 == 0 else g.scalar
        q.dma_start(T.trs[16 * k:16 * k + 16, :, :, :, :], T.tri[:]).then_inc(sem.lt, 16)
    g.sync.dma_start(T.xs[:], T.x[:]).then_inc(sem.lx, 16)
    g.sync.dma_start(T.ws[:, 512:2048], T.w[:, 512:2048]).then_inc(sem.lw, 16)
    g.sync.dma_start(T.vs[:], T.vv[:]).then_inc(sem.lv, 16)
    for k in range(8):
        g.sync.dma_start(T.pls[16 * k:16 * k + 16, :], T.plt[:]).then_inc(sem.lp, 16)
    V.wait_ge(sem.lt, 128)
    for k, (c, d) in enumerate(((1 - p, 0), (1 - p, 1), (p, 0), (p, 1))):
        for q in (0, 1):
            o_x = did(V.tensor_scalar(T.off[:, k, 8 * q:8 * q + 8], T.trs[:, :, c, 2 * d:2 * d + 2, 2 * q:2 * q + 2],
                                      4.0, 0.0, OP.mult, OP.max), "cv")
    V.wait_ge(sem.lw0, 16)
    q_w0 = did(V.quantize_mx(T.wq[:, 0:128], T.wp[:, 0:128], T.ws[:, 0:512]), "cv")

    def gather(s, j, t):
        out, in_ = T.xg[:, 1024 * j + t:1024 * (j + 1):4], T.xs[:, t:2048].indirect(T.off[:, j, :])
        if s == "cv":
            return did(V.tensor_copy(out, in_), "cv")
        return did(A.activation(out, in_, ACT.Copy), "cs")

    for q in (V, A):
        q.wait_ge(sem.lx, 16)
        q.wait_ge(sem.cv, o_x)
    ka = [[gather("cs", j, t) for t in ((2, 3) if j < 2 else (1, 2, 3))][-1] for j in range(4)]
    q_x = []
    for j in range(4):
        kv = [gather("cv", j, t) for t in ((0, 1) if j < 2 else (0,))][-1]
        V.wait_ge(sem.cs, ka[j])
        V.wait_ge(sem.cv, kv)
        q_x.append(did(V.quantize_mx(T.xq[:, 256 * j:256 * j + 256], T.xp[:, 256 * j:256 * j + 256], T.xg[:, 1024 * j:1024 * j + 1024]), "cv"))
        if j == 1:
            V.wait_ge(sem.lw, 16)
            q_w = did(V.quantize_mx(T.wq[:, 128:512], T.wp[:, 128:512], T.ws[:, 512:2048]), "cv")
    V.wait_ge(sem.lv, 16)
    did(V.quantize_mx(T.vq[:], T.vp[:], T.vs[:]), "cv")

    g.wait_ge(sem.cv, q_w0)
    send("w0")
    for d in (0, 1):
        g.wait_ge(sem.cv, q_x[d])
        send("xf%dc" % d, "xf%ds" % d)
    g.wait_ge(sem.cv, q_x[3])
    send("xnc", "xns")
    send("w1", "w2")
    g.sync.wait_ge(sem.cv, q_x[3])
    c, me = 512 + 256 * e + 128 * p + 64 * h, 64 * (2 * h + e)
    g.sync.dma_start(T.nq[:, me:me + 64].bitcast(dt.uint8), T.xq[:, c:c + 64].bitcast(dt.uint8)).then_inc(sem.lo, 16)
    g.sync.dma_start(T.np[:, me:me + 64], T.xp[:, c:c + 64]).then_inc(sem.lo, 16)

    V.wait_ge(sem.lp, 128)
    pt = lambda k: T.pt[:, k, :]

    def bits(k, b, m):
        return did(V.tensor_scalar(pt(k), T.pls[:], b, m, OP.arith_shift_right, OP.bitwise_and), "cv")

    def two(k, i, j, op):
        return did(V.tensor_tensor(pt(k), pt(i), T.pls[:] if j is None else pt(j), op), "cv")

    for k, b, m in ((0, 7, 7), (1, 4, 7), (2, 9, 1), (3, 8, 1)):
        kk = bits(k, b, m)
    V.wait_ge(sem.cv, kk)
    two(4, 1, 0, OP.subtract)
    kk = two(5, 3, 2, OP.subtract)
    V.wait_ge(sem.cv, kk)
    did(V.tensor_scalar(pt(6), pt(4), 112.0, None, OP.mult), "cv")
    kk = did(V.tensor_scalar(pt(7), pt(5), 32.0, None, OP.mult), "cv")
    V.wait_ge(sem.cv, kk)
    kk = two(8, 6, 7, OP.add)
    V.wait_ge(sem.cv, kk)
    kk = two(9, 8, None, OP.add)
    V.wait_ge(sem.cv, kk)
    did(V.tensor_copy(T.yo[:], pt(9)), "cv")

    X.wait_ge(sem.cv, q_w)
    X.wait_ge(sem.lo, 32)
    arrived(X, "jn")
    first_stage("nq", 64 * p, 0)
    arrived(X, "jf")
    first_stage("fq", 64 * (1 - p), 4)
    q_h = pack_h(128)
    g.wait_ge(sem.cv, q_h)
    send("hc", "hs")

    near = [b for b in range(N) if par[b] == p]
    far = [b for b in range(N) if par[b] != p]

    def second_stage(bank, src, c, where):
        k = did(X.matmul_mx(T.ps[:, 512 * bank:512 * bank + 128], T.vq[:], T.vp[:], T[src][:, c:c + 128], T[PLANE[src]][:, c:c + 128], True, True), "ct")
        s = ("cv", "cs")[bank % 2]
        queue[s].wait_ge(sem.ct, k)
        for c0, w, to in where:
            out, in_ = T.ys[:, to:to + w], T.ps[:, 512 * bank + c0:512 * bank + c0 + w]
            if s == "cv":
                did(V.tensor_copy(out, in_), "cv")
            else:
                did(A.activation(out, in_, ACT.Copy), "cs")

    X.wait_ge(sem.cv, q_h)
    X.wait_ge(sem.cs, n["cs"])
    second_stage(0, "hq", 128 * near.index(rank), [(0, 128, 128 * rank)])
    bank = 1
    for s, base, ps in (("y1", 512, 1 - p), ("y0", 0, p), ("y2", 768, p)):
        arrived(X, s)
        if s == "y0":
            for j, a in enumerate(near):
                if a != rank:
                    second_stage(bank, "yq", 128 * j, [(0, 128, 128 * a)])
                    bank += 1
        else:
            for j in (0, 2):
                second_stage(bank, "yq", base + 64 * j, [(64 * i, 64, 128 * far[j + i] + 64 * ps) for i in (0, 1)])
                bank += 1
    for q in (V, A):
        q.wait_ge(sem.cv, n["cv"])
        q.wait_ge(sem.cs, n["cs"])
    kv = did(V.tensor_copy(T.yb[:, 0:256], T.ys[:].indirect(T.yo[:, 0:16])), "cv")
    ks = did(A.activation(T.yb[:, 256:512], T.ys[:].indirect(T.yo[:, 16:32]), ACT.Copy), "cs")
    g.sync.wait_ge(sem.cv, kv)
    g.sync.dma_start(T.y[:, 0:256], T.yb[:, 0:256]).then_inc(sem.ly, 16)
    A.wait_ge(sem.cs, ks)
    A.dma_start(T.y[:, 256:512], T.yb[:, 256:512]).then_inc(sem.ly, 16)
    g.wait_ge(sem.ly, 32)
    finish()
